import numpy as np
import ml_dtypes


def mxq(x, axis, fmt="e4m3"):
    dtype, down = {"e4m3": (ml_dtypes.float8_e4m3fn, 7), "e5m2": (ml_dtypes.float8_e5m2, 14)}[fmt]
    v = np.moveaxis(np.asarray(x, np.float32).astype(ml_dtypes.bfloat16).astype(np.float64), axis, -1)
    blocks = v.reshape(v.shape[:-1] + (-1, 32))
    amax = np.abs(blocks).max(-1, keepdims=True)
    byte = np.maximum(np.where(amax > 0, np.frexp(amax)[1] - 1 + 127, 0) - down, 1)
    scale = np.exp2(byte - 127.0)
    codes = (blocks / scale).astype(np.float32).astype(dtype).astype(np.float64)
    return np.moveaxis((codes * scale).reshape(v.shape), -1, axis)


WIDE = False


def mx_kscale(k):
    if not WIDE:
        return np.ones(k)
    levels = np.array([10, -10, 5, -5, 0])
    if k % 512:
        return np.exp2(np.random.permutation(np.resize(levels, k // 32))).repeat(32)
    a = np.empty((k // 512, 16))
    for p in range(k // 512):
        a[p, :8] = np.random.permutation(np.resize(levels, 8))
        for g in range(8):
            far = levels[np.abs(levels - a[p, g]) >= 10]
            a[p, g + 8] = far[np.random.randint(len(far))]
    return np.exp2(a.ravel()).repeat(32)


def f64(x):
    return np.asarray(x).astype(np.float64)


def striped(idx):
    return np.tile(idx.reshape(-1, 16).T, (8, 1)).astype(np.uint16)


def unstriped(offs):
    return offs[:16].T.reshape(-1).astype(np.int64)


def striped8(idx):
    return np.concatenate([x.reshape(-1, 16).T for x in idx]).astype(np.uint16)


def runs(offs, k):
    lists = np.stack([offs[16 * r : 16 * r + 16].T.reshape(-1) for r in range(8)]).astype(np.int64)
    return lists[np.arange(k) % 512 // 64]


def pack_weight(w):
    k, n = w.shape
    w = f64(np.asarray(w, np.float32).astype(ml_dtypes.bfloat16)).reshape(k // 32, 32, n)
    amax = np.abs(w).max(1)
    byte = np.clip(np.where(amax > 0, np.frexp(amax)[1] - 1 + 127 - 7, 1), 1, 254)
    scaled = (w * np.exp2(127.0 - byte)[:, None, :]).reshape(k, n).astype(np.float32)
    words = np.ascontiguousarray(scaled.reshape(k // 512, 128, 4, n).transpose(0, 1, 3, 2)).astype(ml_dtypes.float8_e4m3fn).view(np.uint8)
    return words, np.ascontiguousarray(byte.astype(np.uint8).reshape(k // 512, 16, n))


def unpack_weight(words, scales):
    g, p, n, _ = words.shape
    vals = np.ascontiguousarray(words).view(ml_dtypes.float8_e4m3fn).astype(np.float64) * np.repeat(np.exp2(scales.astype(np.float64) - 127.0), 8, axis=1)[..., None]
    return vals.transpose(0, 1, 3, 2).reshape(g * 512, n)


def sigmoid(v):
    return 1.0 / (1.0 + np.exp(-np.maximum(v, -700.0)))

def planes(y):
    n, m = y.shape
    v = y.astype(np.float32).astype(ml_dtypes.bfloat16).astype(np.float64).reshape(n // 32, 32, m)
    top = np.abs(v).max(1)
    byte = np.clip(np.where(top > 0, np.frexp(top)[1] - 1 + 127 - 7, 1), 1, 254)
    codes = (v * np.exp2(127.0 - byte)[:, None, :]).reshape(n, m).astype(np.float32).astype(ml_dtypes.float8_e4m3fn).view(np.uint8)
    words = codes.reshape(n // 512, 128, 4, m).transpose(0, 1, 3, 2)
    return np.ascontiguousarray(words), np.ascontiguousarray(byte.astype(np.uint8).reshape(n // 512, 16, m))


K, T, S, N, H, W, G = 512, 2048, 512, 512, 512, 1024, 2048


def setup_inputs():
    n = np.random.standard_normal
    s = mx_kscale(K)[:, None]
    u = mx_kscale(S)
    packed_xT = pack_weight(n((K, T)) * s)
    packed_w1 = pack_weight(n((K, H)) / np.sqrt(K) / s)
    packed_w2 = pack_weight(n((H, N)) / np.sqrt(H) / u[:, None])
    packed_dT = pack_weight(n((K, G)) / s)
    return {
        "x_words": packed_xT[0],
        "x_scales": packed_xT[1],
        "w1_words": packed_w1[0],
        "w1_scales": packed_w1[1],
        "gn": (np.random.uniform(0.5, 1.5, (H, 1)) * u[:, None]).astype(np.float32),
        "w2_words": packed_w2[0],
        "w2_scales": packed_w2[1],
        "d_words": packed_dT[0],
        "d_scales": packed_dT[1],
        "offs": striped(np.random.permutation(T)[:S]),
        "n1": striped(np.random.randint(0, S, W)),
        "two": striped(np.random.permutation(T)[:S]),
        "k1": striped8(np.random.randint(0, G, (8, H))),
        "n2": striped(np.random.permutation(S)),
        "n3": striped(np.random.permutation(S)),
    }


def reference(x_words, x_scales, w1_words, w1_scales, gn, w2_words, w2_scales, d_words, d_scales, offs, n1, two, k1, n2, n3):
    xq = unpack_weight(x_words, x_scales)[:, unstriped(offs)]
    y = unpack_weight(w1_words, w1_scales).T @ xq
    mb = y[:, unstriped(n1)]
    mn = mb.reshape(H, S, 2).min(axis=2)
    mx = mb.reshape(H, S, 2).max(axis=2)
    z = f64(gn) * ((y - mn) * sigmoid(mx))
    a = unpack_weight(w2_words, w2_scales).T @ mxq(z, 0, "e4m3")
    d_k1 = unpack_weight(d_words, d_scales)[np.arange(K)[:, None], runs(k1, K)]
    x_two = unpack_weight(x_words, x_scales)[:, unstriped(two)]
    b = 0.0625 * (d_k1.T @ x_two)
    out_0 = a * (sigmoid(b[:, unstriped(n3)])) - (0.5 * a[:, unstriped(n2)])
    return (out_0,) + planes(out_0)

@@ -1,0 +1,290 @@
+from contextlib import ExitStack
+
+import concourse.mybir as mybir
+
+F32 = mybir.dt.float32
+BF16 = mybir.dt.bfloat16
+I32 = mybir.dt.int32
+U32 = mybir.dt.uint32
+U16 = mybir.dt.uint16
+U8 = mybir.dt.uint8
+FP8X4 = mybir.dt.float8_e4m3fn_x4
+ALU = mybir.AluOpType
+ACT = mybir.ActivationFunctionType
+
+P = 128
+PACK = 4
+S = 512
+TABLE = 2048
+HALF = 256
+QUARTER = 128
+FLOPS = 3 * 2 * 512 * 512 * 512
+
+
+def entries(offsets, first, count):
+    return offsets[:, first // 16 : (first + count) // 16]
+
+
+def words_of(dram_words):
+    return dram_words[0].rearrange("p n t -> p (n t)").bitcast(I32)
+
+
+def deal(copy, dst, src, run):
+    copy(
+        dst.rearrange("p (t b i) -> p b t i", t=PACK, i=run),
+        src.rearrange("p (b i t) -> p b t i", t=PACK, i=run),
+    )
+
+
+def tile_picked_cdjoingatebghard_none_po_kernel(
+    tc, x_words, x_scales, w1_words, w1_scales, gn, w2_words, w2_scales, d_words, d_scales,
+    offs, n1, two, k1, n2, n3, out_0, out_1, out_2,
+):
+    nc = tc.nc
+    with ExitStack() as ctx:
+        keep = ctx.enter_context(tc.tile_pool(name="keep", bufs=1))
+        reuse = ctx.enter_context(tc.tile_pool(name="reuse", bufs=1))
+        ring = ctx.enter_context(tc.tile_pool(name="ring", bufs=2))
+        psum = ctx.enter_context(tc.psum_pool(name="psum", bufs=4))
+
+        def sbuf(name, shape, dtype, tag=None):
+            return keep.tile(shape, dtype, name=name, tag=tag or name, align_bytes=64)
+
+        def placed(name, shape, dtype, offset):
+            return reuse.tile(shape, dtype, name=name, align_bytes=64, offset=offset)
+
+        def load_list(name, dram_list):
+            tile = keep.tile(list(dram_list.shape), U16, name=name)
+            nc.sync.dma_start(tile[:], dram_list)
+            return tile
+
+        def load_scale_rows(queue, tile, dram_scales, quadrants):
+            for q in quadrants:
+                queue.dma_start(tile[32 * q : 32 * q + 4, :].bitcast(I32), dram_scales[0, 4 * q : 4 * q + 4, :].bitcast(I32))
+
+        x_scale_table = sbuf("x_scale_table", [P, TABLE], U8)
+        w1_scale_raw = placed("w1_scale_raw", [P, S], U8, 8192)
+        d_scale_table = sbuf("d_scale_table", [P, TABLE], U8)
+        d_scale = sbuf("d_scale", [P, S], U8)
+        w2_scale_raw = placed("w2_scale_raw", [P, S], U8, 20480)
+        nc.gpsimd.memset(x_scale_table[:, : TABLE // 2].bitcast(I32), 0)
+        nc.vector.memset(x_scale_table[:, TABLE // 2 :].bitcast(I32), 0)
+        nc.vector.memset(d_scale_table[:].bitcast(I32), 0)
+        nc.vector.memset(w1_scale_raw[:].bitcast(I32), 0)
+        nc.vector.memset(w2_scale_raw[:].bitcast(I32), 0)
+        nc.vector.memset(d_scale[:].bitcast(I32), 0)
+
+        offs_sb = load_list("offs_sb", offs)
+        two_sb = load_list("two_sb", two)
+        load_scale_rows(nc.sync, x_scale_table, x_scales, range(2))
+        load_scale_rows(nc.scalar, x_scale_table, x_scales, range(2, 4))
+        x_table = placed("x_table", [P, TABLE], I32, 0)
+        nc.sync.dma_start(x_table[:], words_of(x_words))
+        w1_raw = sbuf("w1_raw", [P, S], I32)
+        nc.sync.dma_start(w1_raw[:], words_of(w1_words))
+        load_scale_rows(nc.sync, w1_scale_raw, w1_scales, range(4))
+        n1_sb = load_list("n1_sb", n1)
+        w2_raw = placed("w2_raw", [P, S], I32, 10240)
+        nc.sync.dma_start(w2_raw[:], words_of(w2_words))
+        k1_sb = load_list("k1_sb", k1)
+        for e in range(2):
+            nc.sync.dma_start(d_scale_table[e:P:16, :].bitcast(I32), d_scales[0, e:16:2, :].bitcast(I32))
+        d_table = placed("d_table", [P, TABLE], I32, 12288)
+        nc.sync.dma_start(d_table[:], words_of(d_words))
+        gain = sbuf("gain", [P, PACK], F32)
+        nc.sync.dma_start(gain[:], gn.rearrange("(p t) o -> p (t o)", t=PACK))
+        load_scale_rows(nc.sync, w2_scale_raw, w2_scales, range(4))
+        n3_sb = load_list("n3_sb", n3)
+        n2_sb = load_list("n2_sb", n2)
+
+        xq_scale = sbuf("xq_scale", [P, S], U8)
+        nc.vector.tensor_copy(xq_scale[:], x_scale_table[:].indirect(offs_sb[:]))
+        xt_scale = sbuf("xt_scale", [P, S], U8)
+        nc.vector.tensor_copy(xt_scale[:], x_scale_table[:].indirect(two_sb[:]))
+        xq = sbuf("xq", [P, S], U32)
+        nc.vector.tensor_copy(xq[:], x_table[:].bitcast(U32).indirect(offs_sb[:]))
+        w1 = sbuf("w1", [P, S], U32)
+        deal(nc.scalar.copy, w1[:], w1_raw[:].bitcast(U32), 4)
+        w1_scale = sbuf("w1_scale", [P, S], U8)
+        deal(nc.vector.tensor_copy, w1_scale[:], w1_scale_raw[:], 16)
+
+        w2 = sbuf("w2", [P, S], U32)
+        deal(nc.scalar.copy, w2[:], w2_raw[:].bitcast(U32), 4)
+
+        def product(bank, t, lhs, lhs_scale, rhs, rhs_scale):
+            cols = slice(P * t, P * (t + 1))
+            nc.tensor.matmul_mx(
+                out=bank, lhsT=lhs[:, cols].bitcast(FP8X4), lhsT_scale=lhs_scale[:, cols],
+                rhs=rhs.bitcast(FP8X4), rhs_scale=rhs_scale, start=True, stop=True,
+            )
+
+        y = []
+        for t in range(PACK):
+            bank = psum.tile([P, S], F32, name="first")
+            product(bank[:], t, w1, w1_scale, xq[:], xq_scale[:])
+            y.append(placed("y0", [P, S], F32, 10240) if t == 0 else sbuf(f"y{t}", [P, S], F32))
+            if t < 2:
+                nc.scalar.copy(y[t][:], bank[:])
+            else:
+                nc.vector.tensor_copy(y[t][:], bank[:])
+
+        xt = placed("xt", [P, S], U32, 8192)
+        nc.vector.tensor_copy(xt[:], x_table[:].bitcast(U32).indirect(two_sb[:]))
+        d_scale_picked = placed("d_scale_picked", [P, S], U8, 0)
+        nc.vector.tensor_copy(d_scale_picked[:], d_scale_table[:].indirect(k1_sb[:]))
+        d_scale_dealt = sbuf("d_scale_dealt", [P, S], U8)
+        deal(nc.vector.tensor_copy, d_scale_dealt[:], d_scale_picked[:], 16)
+        for r in range(4):
+            src = 16 * (r // 2) + r % 2
+            nc.sync.dma_start(d_scale[r:P:32, :].bitcast(I32), d_scale_dealt[src:P:32, :].bitcast(I32))
+        d_picked = sbuf("d_picked", [P, S], U32)
+        nc.vector.tensor_copy(d_picked[:], d_table[:].bitcast(U32).indirect(k1_sb[:]))
+        d_dealt = sbuf("d_dealt", [P, S], I32)
+        deal(nc.vector.tensor_copy, d_dealt[:], d_picked[:].bitcast(I32), 4)
+        w2_scale = placed("w2_scale", [P, S], U8, 512)
+        deal(nc.vector.tensor_copy, w2_scale[:], w2_scale_raw[:], 16)
+
+        members, low, high, gate, diff = {}, {}, {}, {}, {}
+        z_rows = [sbuf(f"z_rows{c}", [P, PACK, HALF], BF16) for c in range(2)]
+
+        def fetch_members(c, u):
+            members[c, u] = ring.tile([P, 2, 2 * HALF], F32, name="members")
+            for e in range(2):
+                for h in range(2):
+                    nc.scalar.activation(
+                        members[c, u][:, e, HALF * h : HALF * (h + 1)],
+                        y[2 * u + e][:].indirect(entries(n1_sb, 2 * HALF * c + HALF * h, HALF)), ACT.Copy,
+                    )
+
+        def extremes(c, u):
+            pair = members[c, u][:].rearrange("p e (j m) -> p (e j) m", m=2)
+            if (c, u) == (0, 1):
+                high[c, u] = placed("high01", [P, 2 * HALF], F32, 12288)
+                low[c, u] = placed("low01", [P, 2 * HALF], F32, 12288 + 2048)
+            else:
+                high[c, u] = sbuf(f"high{c}{u}", [P, 2 * HALF], F32)
+                low[c, u] = sbuf(f"low{c}{u}", [P, 2 * HALF], F32)
+            nc.vector.tensor_tensor(high[c, u][:], pair[:, :, 0], pair[:, :, 1], ALU.max)
+            nc.vector.tensor_tensor(low[c, u][:], pair[:, :, 0], pair[:, :, 1], ALU.min)
+
+        def sigmoid_of_high(c, u):
+            gate[c, u] = sbuf(f"gate{c}{u}", [P, 2 * HALF], F32)
+            nc.scalar.activation(gate[c, u][:], high[c, u][:], ACT.Sigmoid)
+
+        def subtract_low(c, u):
+            if (c, u) == (0, 1):
+                diff[c, u] = placed("diff01", [P, 2 * HALF], F32, 20480)
+            else:
+                diff[c, u] = sbuf(f"diff{c}{u}", [P, 2 * HALF], F32)
+            for e in range(2):
+                part = slice(HALF * e, HALF * (e + 1))
+                nc.vector.tensor_tensor(diff[c, u][:, part], y[2 * u + e][:, HALF * c : HALF * (c + 1)], low[c, u][:, part], ALU.subtract)
+
+        def make_z(c, u):
+            for e in range(2):
+                t, part = 2 * u + e, slice(HALF * e, HALF * (e + 1))
+                nc.vector.scalar_tensor_tensor(z_rows[c][:, t, :], diff[c, u][:, part], gain[:, t : t + 1], gate[c, u][:, part], ALU.mult, ALU.mult)
+
+        z_words, z_scale = {}, {}
+
+        def quantise_z(c):
+            grouped = sbuf(f"z_grouped{c}", [P, HALF, PACK], BF16)
+            nc.vector.tensor_copy(grouped[:], z_rows[c][:].rearrange("p t j -> p j t"))
+            z_words[c] = sbuf(f"z_words{c}", [P, HALF], U32)
+            z_scale[c] = sbuf(f"z_scale{c}", [P, HALF], U8)
+            nc.vector.quantize_mx(out=z_words[c][:].bitcast(FP8X4), scales=z_scale[c][:], in_=grouped[:].rearrange("p j t -> p (j t)"))
+
+        a = [sbuf(f"a{t}", [P, S], F32) for t in range(PACK)]
+        sig_b = [sbuf(f"sig_b{t}", [P, S], F32) for t in range(PACK)]
+        gated = [sbuf(f"gated{c}", [P, PACK, HALF], F32) for c in range(2)]
+
+        def make_a(c, tag):
+            for t in range(PACK):
+                bank = psum.tile([P, HALF], F32, name=tag)
+                product(bank[:], t, w2, w2_scale, z_words[c][:], z_scale[c][:])
+                nc.scalar.copy(a[t][:, HALF * c : HALF * (c + 1)], bank[:])
+
+        def make_sig_b(t):
+            bank = psum.tile([P, S], F32, name="second")
+            product(bank[:], t, d_dealt, d_scale, xt[:], xt_scale[:])
+            nc.scalar.activation(sig_b[t][:], bank[:], ACT.Sigmoid, scale=0.0625)
+
+        def gate_a(c, t):
+            nc.vector.tensor_tensor(
+                gated[c][:, t, :], sig_b[t][:].indirect(entries(n3_sb, HALF * c, HALF)),
+                a[t][:, HALF * c : HALF * (c + 1)], ALU.mult,
+            )
+
+        picked_sig = {}
+
+        def fetch_sig_b(c, t):
+            picked_sig[c, t] = sbuf(f"picked_sig{c}{t}", [P, HALF], F32)
+            nc.scalar.activation(picked_sig[c, t][:], sig_b[t][:].indirect(entries(n3_sb, HALF * c, HALF)), ACT.Copy)
+
+        def gate_a_fetched(c, t):
+            nc.vector.tensor_tensor(gated[c][:, t, :], picked_sig[c, t][:], a[t][:, HALF * c : HALF * (c + 1)], ALU.mult)
+
+        steps = [(c, u) for c in range(2) for u in range(2)]
+        for i in range(len(steps) + 1):
+            if i < len(steps):
+                fetch_members(*steps[i])
+            if i >= 1:
+                sigmoid_of_high(*steps[i - 1])
+            if i < len(steps):
+                extremes(*steps[i])
+            if i >= 1:
+                make_z(*steps[i - 1])
+            if i < len(steps):
+                subtract_low(*steps[i])
+            if i == 2:
+                quantise_z(0)
+        for t in range(PACK):
+            make_sig_b(t)
+        make_a(0, "first")
+        quantise_z(1)
+        for t in range(PACK):
+            gate_a(0, t)
+        fetch_sig_b(1, 0)
+        make_a(1, "second")
+        gate_a_fetched(1, 0)
+        for t in range(1, PACK):
+            gate_a(1, t)
+
+        out_rows = out_0.rearrange("(p t) j -> p t j", t=PACK)
+        out_words = sbuf("out_words", [P, S], U32)
+        out_scale = sbuf("out_scale", [P, S], U8)
+        out_words_dram = words_of(out_1)
+        result = {}
+
+        def combine(c):
+            fetched = sbuf(f"fetched{c}", [P, PACK, QUARTER], F32)
+            for t in range(PACK):
+                nc.scalar.activation(fetched[:, t, :], a[t][:].indirect(entries(n2_sb, QUARTER * c, QUARTER)), ACT.Copy)
+            result[c] = sbuf(f"result{c}", [P, PACK, QUARTER], F32)
+            part = slice(QUARTER * (c % 2), QUARTER * (c % 2 + 1))
+            nc.vector.scalar_tensor_tensor(result[c][:], fetched[:], -0.5, gated[c // 2][:, :, part], ALU.mult, ALU.add)
+            nc.sync.dma_start(out_rows[:, :, QUARTER * c : QUARTER * (c + 1)], result[c][:])
+
+        grouped_out = {}
+
+        def group_out(c):
+            grouped_out[c] = sbuf(f"out_grouped{c}", [P, QUARTER, PACK], BF16)
+            nc.vector.tensor_copy(grouped_out[c][:], result[c][:].rearrange("p t j -> p j t"))
+
+        def quantise_out(c):
+            cols = slice(QUARTER * c, QUARTER * (c + 1))
+            nc.vector.quantize_mx(out=out_words[:, cols].bitcast(FP8X4), scales=out_scale[:, cols], in_=grouped_out[c][:].rearrange("p j t -> p (j t)"))
+            if c % 2 == 1:
+                half = slice(HALF * (c // 2), HALF * (c // 2 + 1))
+                nc.sync.dma_start(out_words_dram[:, half], out_words[:, half].bitcast(I32))
+
+        for c in range(4 + 1):
+            if c < 4:
+                combine(c)
+            if c >= 1:
+                quantise_out(c - 1)
+            if c < 4:
+                group_out(c)
+        for q in range(4):
+            queue = nc.scalar if q % 2 == 0 else nc.sync
+            queue.dma_start(out_2[0, 4 * q : 4 * q + 4, :].bitcast(I32), out_scale[32 * q : 32 * q + 4, :].bitcast(I32))

@@ -73,6 +73,8 @@ def tile_picked_cdjoingatebghard_none_po_kernel(
         nc.vector.memset(w1_scale_raw[:].bitcast(I32), 0)
         nc.vector.memset(w2_scale_raw[:].bitcast(I32), 0)
         nc.vector.memset(d_scale[:].bitcast(I32), 0)
+        warm = sbuf("warm", [P, 16], F32)
+        nc.vector.memset(warm[:, 0:1], 0.0)
 
         offs_sb = load_list("offs_sb", offs)
         two_sb = load_list("two_sb", two)
@@ -97,6 +99,7 @@ def tile_picked_cdjoingatebghard_none_po_kernel(
         n3_sb = load_list("n3_sb", n3)
         n2_sb = load_list("n2_sb", n2)
 
+        nc.scalar.activation(warm[:, 8:9], warm[:, 0:1], ACT.Sigmoid)
         xq_scale = sbuf("xq_scale", [P, S], U8)
         nc.vector.tensor_copy(xq_scale[:], x_scale_table[:].indirect(offs_sb[:]))
         xt_scale = sbuf("xt_scale", [P, S], U8)

@@ -36,6 +36,13 @@ def deal(copy, dst, src, run):
     )
 
 
+def interleave(nc, dst, src):
+    nc.vector.tensor_copy(
+        dst.rearrange("p (b i) t -> p b t i", i=4),
+        src.rearrange("p t (b i) -> p b t i", i=4),
+    )
+
+
 def tile_picked_cdjoingatebghard_none_po_kernel(
     tc, x_words, x_scales, w1_words, w1_scales, gn, w2_words, w2_scales, d_words, d_scales,
     offs, n1, two, k1, n2, n3, out_0, out_1, out_2,
@@ -44,7 +51,6 @@ def tile_picked_cdjoingatebghard_none_po_kernel(
     with ExitStack() as ctx:
         keep = ctx.enter_context(tc.tile_pool(name="keep", bufs=1))
         reuse = ctx.enter_context(tc.tile_pool(name="reuse", bufs=1))
-        ring = ctx.enter_context(tc.tile_pool(name="ring", bufs=2))
         psum = ctx.enter_context(tc.psum_pool(name="psum", bufs=4))
 
         def sbuf(name, shape, dtype, tag=None):
@@ -64,7 +70,7 @@ def tile_picked_cdjoingatebghard_none_po_kernel(
 
         x_scale_table = sbuf("x_scale_table", [P, TABLE], U8)
         w1_scale_raw = placed("w1_scale_raw", [P, S], U8, 8192)
-        d_scale_table = sbuf("d_scale_table", [P, TABLE], U8)
+        d_scale_table = placed("d_scale_table", [P, TABLE], U8, 41984)
         d_scale = sbuf("d_scale", [P, S], U8)
         w2_scale_raw = placed("w2_scale_raw", [P, S], U8, 20480)
         nc.gpsimd.memset(x_scale_table[:, : TABLE // 2].bitcast(I32), 0)
@@ -85,9 +91,9 @@ def tile_picked_cdjoingatebghard_none_po_kernel(
         w1_raw = sbuf("w1_raw", [P, S], I32)
         nc.sync.dma_start(w1_raw[:], words_of(w1_words))
         load_scale_rows(nc.sync, w1_scale_raw, w1_scales, range(4))
-        n1_sb = load_list("n1_sb", n1)
-        w2_raw = placed("w2_raw", [P, S], I32, 10240)
+        w2_raw = placed("w2_raw", [P, S], I32, 37888)
         nc.sync.dma_start(w2_raw[:], words_of(w2_words))
+        n1_sb = load_list("n1_sb", n1)
         k1_sb = load_list("k1_sb", k1)
         for e in range(2):
             nc.sync.dma_start(d_scale_table[e:P:16, :].bitcast(I32), d_scales[0, e:16:2, :].bitcast(I32))
@@ -121,16 +127,6 @@ def tile_picked_cdjoingatebghard_none_po_kernel(
                 rhs=rhs.bitcast(FP8X4), rhs_scale=rhs_scale, start=True, stop=True,
             )
 
-        y = []
-        for t in range(PACK):
-            bank = psum.tile([P, S], F32, name="first")
-            product(bank[:], t, w1, w1_scale, xq[:], xq_scale[:])
-            y.append(placed("y0", [P, S], F32, 10240) if t == 0 else sbuf(f"y{t}", [P, S], F32))
-            if t < 2:
-                nc.scalar.copy(y[t][:], bank[:])
-            else:
-                nc.vector.tensor_copy(y[t][:], bank[:])
-
         xt = placed("xt", [P, S], U32, 8192)
         nc.vector.tensor_copy(xt[:], x_table[:].bitcast(U32).indirect(two_sb[:]))
         d_scale_picked = placed("d_scale_picked", [P, S], U8, 0)
@@ -140,6 +136,16 @@ def tile_picked_cdjoingatebghard_none_po_kernel(
         for r in range(4):
             src = 16 * (r // 2) + r % 2
             nc.sync.dma_start(d_scale[r:P:32, :].bitcast(I32), d_scale_dealt[src:P:32, :].bitcast(I32))
+        y = []
+        for t in range(PACK):
+            bank = psum.tile([P, S], F32, name="first")
+            product(bank[:], t, w1, w1_scale, xq[:], xq_scale[:])
+            y.append(placed(f"y{t}", [P, S], F32, 36864 + 2048 * t))
+            if t < 2:
+                nc.scalar.copy(y[t][:], bank[:])
+            else:
+                nc.vector.tensor_copy(y[t][:], bank[:])
+
         d_picked = sbuf("d_picked", [P, S], U32)
         nc.vector.tensor_copy(d_picked[:], d_table[:].bitcast(U32).indirect(k1_sb[:]))
         d_dealt = sbuf("d_dealt", [P, S], I32)
@@ -151,7 +157,7 @@ def tile_picked_cdjoingatebghard_none_po_kernel(
         z_rows = [sbuf(f"z_rows{c}", [P, PACK, HALF], BF16) for c in range(2)]
 
         def fetch_members(c, u):
-            members[c, u] = ring.tile([P, 2, 2 * HALF], F32, name="members")
+            members[c, u] = placed(f"members{c}{u}", [P, 2, 2 * HALF], F32, 22528 + 4096 * u)
             for e in range(2):
                 for h in range(2):
                     nc.scalar.activation(
@@ -161,7 +167,7 @@ def tile_picked_cdjoingatebghard_none_po_kernel(
 
         def extremes(c, u):
             pair = members[c, u][:].rearrange("p e (j m) -> p (e j) m", m=2)
-            if (c, u) == (0, 1):
+            if (c, u) == (0, 0):
                 high[c, u] = placed("high01", [P, 2 * HALF], F32, 12288)
                 low[c, u] = placed("low01", [P, 2 * HALF], F32, 12288 + 2048)
             else:
@@ -191,15 +197,15 @@ def tile_picked_cdjoingatebghard_none_po_kernel(
         z_words, z_scale = {}, {}
 
         def quantise_z(c):
-            grouped = sbuf(f"z_grouped{c}", [P, HALF, PACK], BF16)
-            nc.vector.tensor_copy(grouped[:], z_rows[c][:].rearrange("p t j -> p j t"))
+            grouped = placed(f"z_grouped{c}", [P, HALF, PACK], BF16, 30720)
+            interleave(nc, grouped[:], z_rows[c][:])
             z_words[c] = sbuf(f"z_words{c}", [P, HALF], U32)
             z_scale[c] = sbuf(f"z_scale{c}", [P, HALF], U8)
             nc.vector.quantize_mx(out=z_words[c][:].bitcast(FP8X4), scales=z_scale[c][:], in_=grouped[:].rearrange("p j t -> p (j t)"))
 
         a = [sbuf(f"a{t}", [P, S], F32) for t in range(PACK)]
-        sig_b = [sbuf(f"sig_b{t}", [P, S], F32) for t in range(PACK)]
-        gated = [sbuf(f"gated{c}", [P, PACK, HALF], F32) for c in range(2)]
+        sig_b = {}
+        gated = {}
 
         def make_a(c, tag):
             for t in range(PACK):
@@ -210,6 +216,7 @@ def tile_picked_cdjoingatebghard_none_po_kernel(
         def make_sig_b(t):
             bank = psum.tile([P, S], F32, name="second")
             product(bank[:], t, d_dealt, d_scale, xt[:], xt_scale[:])
+            sig_b[t] = placed(f"sig_b{t}", [P, S], F32, 22528 + 2048 * t)
             nc.scalar.activation(sig_b[t][:], bank[:], ACT.Sigmoid, scale=0.0625)
 
         def gate_a(c, t):
@@ -245,13 +252,17 @@ def tile_picked_cdjoingatebghard_none_po_kernel(
             make_sig_b(t)
         make_a(0, "first")
         quantise_z(1)
+        gated[0] = placed("gated0", [P, PACK, HALF], F32, 30720)
+        gated[1] = sbuf("gated1", [P, PACK, HALF], F32)
         for t in range(PACK):
             gate_a(0, t)
         fetch_sig_b(1, 0)
         make_a(1, "second")
-        gate_a_fetched(1, 0)
-        for t in range(1, PACK):
-            gate_a(1, t)
+        for t in range(1, 3):
+            fetch_sig_b(1, t)
+        for t in range(3):
+            gate_a_fetched(1, t)
+        gate_a(1, 3)
 
         out_rows = out_0.rearrange("(p t) j -> p t j", t=PACK)
         out_words = sbuf("out_words", [P, S], U32)
@@ -272,7 +283,7 @@ def tile_picked_cdjoingatebghard_none_po_kernel(
 
         def group_out(c):
             grouped_out[c] = sbuf(f"out_grouped{c}", [P, QUARTER, PACK], BF16)
-            nc.vector.tensor_copy(grouped_out[c][:], result[c][:].rearrange("p t j -> p j t"))
+            interleave(nc, grouped_out[c][:], result[c][:])
 
         def quantise_out(c):
             cols = slice(QUARTER * c, QUARTER * (c + 1))

@@ -86,7 +86,7 @@ def tile_picked_cdjoingatebghard_none_po_kernel(
         two_sb = load_list("two_sb", two)
         load_scale_rows(nc.sync, x_scale_table, x_scales, range(2))
         load_scale_rows(nc.scalar, x_scale_table, x_scales, range(2, 4))
-        x_table = placed("x_table", [P, TABLE], I32, 0)
+        x_table = sbuf("x_table", [P, TABLE], I32)
         nc.sync.dma_start(x_table[:], words_of(x_words))
         w1_raw = sbuf("w1_raw", [P, S], I32)
         nc.sync.dma_start(w1_raw[:], words_of(w1_words))
@@ -129,7 +129,7 @@ def tile_picked_cdjoingatebghard_none_po_kernel(
 
         xt = placed("xt", [P, S], U32, 8192)
         nc.vector.tensor_copy(xt[:], x_table[:].bitcast(U32).indirect(two_sb[:]))
-        d_scale_picked = placed("d_scale_picked", [P, S], U8, 0)
+        d_scale_picked = sbuf("d_scale_picked", [P, S], U8)
         nc.vector.tensor_copy(d_scale_picked[:], d_scale_table[:].indirect(k1_sb[:]))
         d_scale_dealt = sbuf("d_scale_dealt", [P, S], U8)
         deal(nc.vector.tensor_copy, d_scale_dealt[:], d_scale_picked[:], 16)
@@ -150,7 +150,7 @@ def tile_picked_cdjoingatebghard_none_po_kernel(
         nc.vector.tensor_copy(d_picked[:], d_table[:].bitcast(U32).indirect(k1_sb[:]))
         d_dealt = sbuf("d_dealt", [P, S], I32)
         deal(nc.vector.tensor_copy, d_dealt[:], d_picked[:].bitcast(I32), 4)
-        w2_scale = placed("w2_scale", [P, S], U8, 512)
+        w2_scale = sbuf("w2_scale", [P, S], U8)
         deal(nc.vector.tensor_copy, w2_scale[:], w2_scale_raw[:], 16)
 
         members, low, high, gate, diff = {}, {}, {}, {}, {}
@@ -167,9 +167,9 @@ def tile_picked_cdjoingatebghard_none_po_kernel(
 
         def extremes(c, u):
             pair = members[c, u][:].rearrange("p e (j m) -> p (e j) m", m=2)
-            if (c, u) == (0, 0):
-                high[c, u] = placed("high01", [P, 2 * HALF], F32, 12288)
-                low[c, u] = placed("low01", [P, 2 * HALF], F32, 12288 + 2048)
+            if c == 0:
+                high[c, u] = placed(f"high{c}{u}", [P, 2 * HALF], F32, 12288 + 4096 * u)
+                low[c, u] = placed(f"low{c}{u}", [P, 2 * HALF], F32, 12288 + 4096 * u + 2048)
             else:
                 high[c, u] = sbuf(f"high{c}{u}", [P, 2 * HALF], F32)
                 low[c, u] = sbuf(f"low{c}{u}", [P, 2 * HALF], F32)

@@ -16,9 +16,22 @@ P = 128
 PACK = 4
 S = 512
 TABLE = 2048
-HALF = 256
-QUARTER = 128
-FLOPS = 3 * 2 * 512 * 512 * 512
+HALF = S // 2
+QUARTER = S // 4
+WORDS_PER_LINE = 4
+BYTES_PER_LINE = 16
+N3_ON_SCALAR = 2
+
+FLOPS = 3 * 2 * S * S * S
+
+AT_W1_SCALE_RAW = 0
+AT_D_TABLE = 2 * 1024
+AT_W2_SCALE_RAW = 10 * 1024
+AT_MEMBERS = 12 * 1024
+AT_Z_GROUPED = 20 * 1024
+AT_Y = 24 * 1024
+AT_W2_RAW = AT_Y + 1024
+AT_D_SCALE_TABLE = AT_Y + 5 * 1024
 
 
 def entries(offsets, first, count):
@@ -51,10 +64,10 @@ def tile_picked_cdjoingatebghard_none_po_kernel(
     with ExitStack() as ctx:
         keep = ctx.enter_context(tc.tile_pool(name="keep", bufs=1))
         reuse = ctx.enter_context(tc.tile_pool(name="reuse", bufs=1))
-        psum = ctx.enter_context(tc.psum_pool(name="psum", bufs=4))
+        psum = ctx.enter_context(tc.psum_pool(name="psum", bufs=PACK))
 
-        def sbuf(name, shape, dtype, tag=None):
-            return keep.tile(shape, dtype, name=name, tag=tag or name, align_bytes=64)
+        def sbuf(name, shape, dtype):
+            return keep.tile(shape, dtype, name=name, tag=name, align_bytes=64)
 
         def placed(name, shape, dtype, offset):
             return reuse.tile(shape, dtype, name=name, align_bytes=64, offset=offset)
@@ -69,10 +82,10 @@ def tile_picked_cdjoingatebghard_none_po_kernel(
                 queue.dma_start(tile[32 * q : 32 * q + 4, :].bitcast(I32), dram_scales[0, 4 * q : 4 * q + 4, :].bitcast(I32))
 
         x_scale_table = sbuf("x_scale_table", [P, TABLE], U8)
-        w1_scale_raw = placed("w1_scale_raw", [P, S], U8, 8192)
-        d_scale_table = placed("d_scale_table", [P, TABLE], U8, 41984)
+        w1_scale_raw = placed("w1_scale_raw", [P, S], U8, AT_W1_SCALE_RAW)
+        d_scale_table = placed("d_scale_table", [P, TABLE], U8, AT_D_SCALE_TABLE)
         d_scale = sbuf("d_scale", [P, S], U8)
-        w2_scale_raw = placed("w2_scale_raw", [P, S], U8, 20480)
+        w2_scale_raw = placed("w2_scale_raw", [P, S], U8, AT_W2_SCALE_RAW)
         nc.gpsimd.memset(x_scale_table[:, : TABLE // 2].bitcast(I32), 0)
         nc.vector.memset(x_scale_table[:, TABLE // 2 :].bitcast(I32), 0)
         nc.vector.memset(d_scale_table[:].bitcast(I32), 0)
@@ -91,13 +104,13 @@ def tile_picked_cdjoingatebghard_none_po_kernel(
         w1_raw = sbuf("w1_raw", [P, S], I32)
         nc.sync.dma_start(w1_raw[:], words_of(w1_words))
         load_scale_rows(nc.sync, w1_scale_raw, w1_scales, range(4))
-        w2_raw = placed("w2_raw", [P, S], I32, 37888)
+        w2_raw = placed("w2_raw", [P, S], I32, AT_W2_RAW)
         nc.sync.dma_start(w2_raw[:], words_of(w2_words))
         n1_sb = load_list("n1_sb", n1)
         k1_sb = load_list("k1_sb", k1)
         for e in range(2):
             nc.sync.dma_start(d_scale_table[e:P:16, :].bitcast(I32), d_scales[0, e:16:2, :].bitcast(I32))
-        d_table = placed("d_table", [P, TABLE], I32, 12288)
+        d_table = placed("d_table", [P, TABLE], I32, AT_D_TABLE)
         nc.sync.dma_start(d_table[:], words_of(d_words))
         gain = sbuf("gain", [P, PACK], F32)
         nc.sync.dma_start(gain[:], gn.rearrange("(p t) o -> p (t o)", t=PACK))
@@ -106,6 +119,7 @@ def tile_picked_cdjoingatebghard_none_po_kernel(
         n2_sb = load_list("n2_sb", n2)
 
         nc.scalar.activation(warm[:, 8:9], warm[:, 0:1], ACT.Sigmoid)
+
         xq_scale = sbuf("xq_scale", [P, S], U8)
         nc.vector.tensor_copy(xq_scale[:], x_scale_table[:].indirect(offs_sb[:]))
         xt_scale = sbuf("xt_scale", [P, S], U8)
@@ -113,12 +127,21 @@ def tile_picked_cdjoingatebghard_none_po_kernel(
         xq = sbuf("xq", [P, S], U32)
         nc.vector.tensor_copy(xq[:], x_table[:].bitcast(U32).indirect(offs_sb[:]))
         w1 = sbuf("w1", [P, S], U32)
-        deal(nc.scalar.copy, w1[:], w1_raw[:].bitcast(U32), 4)
+        deal(nc.scalar.copy, w1[:], w1_raw[:].bitcast(U32), WORDS_PER_LINE)
         w1_scale = sbuf("w1_scale", [P, S], U8)
-        deal(nc.vector.tensor_copy, w1_scale[:], w1_scale_raw[:], 16)
-
+        deal(nc.vector.tensor_copy, w1_scale[:], w1_scale_raw[:], BYTES_PER_LINE)
         w2 = sbuf("w2", [P, S], U32)
-        deal(nc.scalar.copy, w2[:], w2_raw[:].bitcast(U32), 4)
+        deal(nc.scalar.copy, w2[:], w2_raw[:].bitcast(U32), WORDS_PER_LINE)
+        xt = placed("xt", [P, S], U32, AT_W1_SCALE_RAW)
+        nc.vector.tensor_copy(xt[:], x_table[:].bitcast(U32).indirect(two_sb[:]))
+
+        d_scale_picked = sbuf("d_scale_picked", [P, S], U8)
+        nc.vector.tensor_copy(d_scale_picked[:], d_scale_table[:].indirect(k1_sb[:]))
+        d_scale_dealt = sbuf("d_scale_dealt", [P, S], U8)
+        deal(nc.vector.tensor_copy, d_scale_dealt[:], d_scale_picked[:], BYTES_PER_LINE)
+        for r in range(4):
+            gathered_on = 16 * (r // 2) + r % 2
+            nc.sync.dma_start(d_scale[r:P:32, :].bitcast(I32), d_scale_dealt[gathered_on:P:32, :].bitcast(I32))
 
         def product(bank, t, lhs, lhs_scale, rhs, rhs_scale):
             cols = slice(P * t, P * (t + 1))
@@ -127,21 +150,12 @@ def tile_picked_cdjoingatebghard_none_po_kernel(
                 rhs=rhs.bitcast(FP8X4), rhs_scale=rhs_scale, start=True, stop=True,
             )
 
-        xt = placed("xt", [P, S], U32, 8192)
-        nc.vector.tensor_copy(xt[:], x_table[:].bitcast(U32).indirect(two_sb[:]))
-        d_scale_picked = sbuf("d_scale_picked", [P, S], U8)
-        nc.vector.tensor_copy(d_scale_picked[:], d_scale_table[:].indirect(k1_sb[:]))
-        d_scale_dealt = sbuf("d_scale_dealt", [P, S], U8)
-        deal(nc.vector.tensor_copy, d_scale_dealt[:], d_scale_picked[:], 16)
-        for r in range(4):
-            src = 16 * (r // 2) + r % 2
-            nc.sync.dma_start(d_scale[r:P:32, :].bitcast(I32), d_scale_dealt[src:P:32, :].bitcast(I32))
         y = []
         for t in range(PACK):
             bank = psum.tile([P, S], F32, name="first")
             product(bank[:], t, w1, w1_scale, xq[:], xq_scale[:])
-            y.append(placed(f"y{t}", [P, S], F32, 36864 + 2048 * t))
-            if t < 2:
+            y.append(placed(f"y{t}", [P, S], F32, AT_Y + 2048 * t))
+            if t < PACK // 2:
                 nc.scalar.copy(y[t][:], bank[:])
             else:
                 nc.vector.tensor_copy(y[t][:], bank[:])
@@ -149,15 +163,15 @@ def tile_picked_cdjoingatebghard_none_po_kernel(
         d_picked = sbuf("d_picked", [P, S], U32)
         nc.vector.tensor_copy(d_picked[:], d_table[:].bitcast(U32).indirect(k1_sb[:]))
         d_dealt = sbuf("d_dealt", [P, S], I32)
-        deal(nc.vector.tensor_copy, d_dealt[:], d_picked[:].bitcast(I32), 4)
+        deal(nc.vector.tensor_copy, d_dealt[:], d_picked[:].bitcast(I32), WORDS_PER_LINE)
         w2_scale = sbuf("w2_scale", [P, S], U8)
-        deal(nc.vector.tensor_copy, w2_scale[:], w2_scale_raw[:], 16)
+        deal(nc.vector.tensor_copy, w2_scale[:], w2_scale_raw[:], BYTES_PER_LINE)
 
         members, low, high, gate, diff = {}, {}, {}, {}, {}
         z_rows = [sbuf(f"z_rows{c}", [P, PACK, HALF], BF16) for c in range(2)]
 
         def fetch_members(c, u):
-            members[c, u] = placed(f"members{c}{u}", [P, 2, 2 * HALF], F32, 22528 + 4096 * u)
+            members[c, u] = placed(f"members{c}{u}", [P, 2, 2 * HALF], F32, AT_MEMBERS + 4096 * u)
             for e in range(2):
                 for h in range(2):
                     nc.scalar.activation(
@@ -168,8 +182,8 @@ def tile_picked_cdjoingatebghard_none_po_kernel(
         def extremes(c, u):
             pair = members[c, u][:].rearrange("p e (j m) -> p (e j) m", m=2)
             if c == 0:
-                high[c, u] = placed(f"high{c}{u}", [P, 2 * HALF], F32, 12288 + 4096 * u)
-                low[c, u] = placed(f"low{c}{u}", [P, 2 * HALF], F32, 12288 + 4096 * u + 2048)
+                high[c, u] = placed(f"high{c}{u}", [P, 2 * HALF], F32, AT_D_TABLE + 4096 * u)
+                low[c, u] = placed(f"low{c}{u}", [P, 2 * HALF], F32, AT_D_TABLE + 4096 * u + 2048)
             else:
                 high[c, u] = sbuf(f"high{c}{u}", [P, 2 * HALF], F32)
                 low[c, u] = sbuf(f"low{c}{u}", [P, 2 * HALF], F32)
@@ -182,7 +196,7 @@ def tile_picked_cdjoingatebghard_none_po_kernel(
 
         def subtract_low(c, u):
             if (c, u) == (0, 1):
-                diff[c, u] = placed("diff01", [P, 2 * HALF], F32, 20480)
+                diff[c, u] = placed("diff01", [P, 2 * HALF], F32, AT_W2_SCALE_RAW)
             else:
                 diff[c, u] = sbuf(f"diff{c}{u}", [P, 2 * HALF], F32)
             for e in range(2):
@@ -197,35 +211,32 @@ def tile_picked_cdjoingatebghard_none_po_kernel(
         z_words, z_scale = {}, {}
 
         def quantise_z(c):
-            grouped = placed(f"z_grouped{c}", [P, HALF, PACK], BF16, 30720)
+            grouped = placed(f"z_grouped{c}", [P, HALF, PACK], BF16, AT_Z_GROUPED)
             interleave(nc, grouped[:], z_rows[c][:])
             z_words[c] = sbuf(f"z_words{c}", [P, HALF], U32)
             z_scale[c] = sbuf(f"z_scale{c}", [P, HALF], U8)
             nc.vector.quantize_mx(out=z_words[c][:].bitcast(FP8X4), scales=z_scale[c][:], in_=grouped[:].rearrange("p j t -> p (j t)"))
 
         a = [sbuf(f"a{t}", [P, S], F32) for t in range(PACK)]
-        sig_b = {}
-        gated = {}
+        sig_b, picked_sig, gated = {}, {}, {}
 
-        def make_a(c, tag):
+        def make_a(c, bank_tag):
             for t in range(PACK):
-                bank = psum.tile([P, HALF], F32, name=tag)
+                bank = psum.tile([P, HALF], F32, name=bank_tag)
                 product(bank[:], t, w2, w2_scale, z_words[c][:], z_scale[c][:])
                 nc.scalar.copy(a[t][:, HALF * c : HALF * (c + 1)], bank[:])
 
         def make_sig_b(t):
             bank = psum.tile([P, S], F32, name="second")
             product(bank[:], t, d_dealt, d_scale, xt[:], xt_scale[:])
-            sig_b[t] = placed(f"sig_b{t}", [P, S], F32, 22528 + 2048 * t)
+            sig_b[t] = placed(f"sig_b{t}", [P, S], F32, AT_MEMBERS + 2048 * t)
             nc.scalar.activation(sig_b[t][:], bank[:], ACT.Sigmoid, scale=0.0625)
 
-        def gate_a(c, t):
+        def gate_a_fused(c, t):
             nc.vector.tensor_tensor(
                 gated[c][:, t, :], sig_b[t][:].indirect(entries(n3_sb, HALF * c, HALF)),
                 a[t][:, HALF * c : HALF * (c + 1)], ALU.mult,
             )
-
-        picked_sig = {}
 
         def fetch_sig_b(c, t):
             picked_sig[c, t] = sbuf(f"picked_sig{c}{t}", [P, HALF], F32)
@@ -246,59 +257,63 @@ def tile_picked_cdjoingatebghard_none_po_kernel(
                 make_z(*steps[i - 1])
             if i < len(steps):
                 subtract_low(*steps[i])
-            if i == 2:
+            if i >= 1 and steps[i - 1] == (0, 1):
                 quantise_z(0)
         for t in range(PACK):
             make_sig_b(t)
         make_a(0, "first")
         quantise_z(1)
-        gated[0] = placed("gated0", [P, PACK, HALF], F32, 30720)
+
+        gated[0] = placed("gated0", [P, PACK, HALF], F32, AT_Z_GROUPED)
         gated[1] = sbuf("gated1", [P, PACK, HALF], F32)
         for t in range(PACK):
-            gate_a(0, t)
+            gate_a_fused(0, t)
         fetch_sig_b(1, 0)
         make_a(1, "second")
-        for t in range(1, 3):
+        for t in range(1, N3_ON_SCALAR):
             fetch_sig_b(1, t)
-        for t in range(3):
+        for t in range(N3_ON_SCALAR):
             gate_a_fetched(1, t)
-        gate_a(1, 3)
+        for t in range(N3_ON_SCALAR, PACK):
+            gate_a_fused(1, t)
 
         out_rows = out_0.rearrange("(p t) j -> p t j", t=PACK)
         out_words = sbuf("out_words", [P, S], U32)
         out_scale = sbuf("out_scale", [P, S], U8)
         out_words_dram = words_of(out_1)
-        result = {}
+        result, out_grouped = {}, {}
+        quarters = S // QUARTER
 
-        def combine(c):
-            fetched = sbuf(f"fetched{c}", [P, PACK, QUARTER], F32)
+        def combine(v):
+            fetched = sbuf(f"fetched{v}", [P, PACK, QUARTER], F32)
             for t in range(PACK):
-                nc.scalar.activation(fetched[:, t, :], a[t][:].indirect(entries(n2_sb, QUARTER * c, QUARTER)), ACT.Copy)
-            result[c] = sbuf(f"result{c}", [P, PACK, QUARTER], F32)
-            part = slice(QUARTER * (c % 2), QUARTER * (c % 2 + 1))
-            nc.vector.scalar_tensor_tensor(result[c][:], fetched[:], -0.5, gated[c // 2][:, :, part], ALU.mult, ALU.add)
-            nc.sync.dma_start(out_rows[:, :, QUARTER * c : QUARTER * (c + 1)], result[c][:])
+                nc.scalar.activation(fetched[:, t, :], a[t][:].indirect(entries(n2_sb, QUARTER * v, QUARTER)), ACT.Copy)
+            result[v] = sbuf(f"result{v}", [P, PACK, QUARTER], F32)
+            part = slice(QUARTER * (v % 2), QUARTER * (v % 2 + 1))
+            nc.vector.scalar_tensor_tensor(result[v][:], fetched[:], -0.5, gated[v // 2][:, :, part], ALU.mult, ALU.add)
+            nc.sync.dma_start(out_rows[:, :, QUARTER * v : QUARTER * (v + 1)], result[v][:])
 
-        grouped_out = {}
+        def group_out(v):
+            out_grouped[v] = sbuf(f"out_grouped{v}", [P, QUARTER, PACK], BF16)
+            if v == quarters - 2:
+                nc.scalar.copy(out_grouped[v][:], result[v][:].rearrange("p t j -> p j t"))
+            else:
+                interleave(nc, out_grouped[v][:], result[v][:])
 
-        def group_out(c):
-            grouped_out[c] = sbuf(f"out_grouped{c}", [P, QUARTER, PACK], BF16)
-            interleave(nc, grouped_out[c][:], result[c][:])
-
-        def quantise_out(c):
-            cols = slice(QUARTER * c, QUARTER * (c + 1))
-            nc.vector.quantize_mx(out=out_words[:, cols].bitcast(FP8X4), scales=out_scale[:, cols], in_=grouped_out[c][:].rearrange("p j t -> p (j t)"))
-            if c % 2 == 1:
-                half = slice(HALF * (c // 2), HALF * (c // 2 + 1))
+        def quantise_out(v):
+            cols = slice(QUARTER * v, QUARTER * (v + 1))
+            nc.vector.quantize_mx(out=out_words[:, cols].bitcast(FP8X4), scales=out_scale[:, cols], in_=out_grouped[v][:].rearrange("p j t -> p (j t)"))
+            if v % 2 == 1:
+                half = slice(HALF * (v // 2), HALF * (v // 2 + 1))
                 nc.sync.dma_start(out_words_dram[:, half], out_words[:, half].bitcast(I32))
 
-        for c in range(4 + 1):
-            if c < 4:
-                combine(c)
-            if c >= 1:
-                quantise_out(c - 1)
-            if c < 4:
-                group_out(c)
+        for v in range(quarters + 1):
+            if v < quarters:
+                combine(v)
+            if v >= 1:
+                quantise_out(v - 1)
+            if v < quarters:
+                group_out(v)
         for q in range(4):
             queue = nc.scalar if q % 2 == 0 else nc.sync
             queue.dma_start(out_2[0, 4 * q : 4 * q + 4, :].bitcast(I32), out_scale[32 * q : 32 * q + 4, :].bitcast(I32))

from contextlib import ExitStack

import concourse.mybir as mybir

F32 = mybir.dt.float32
BF16 = mybir.dt.bfloat16
I32 = mybir.dt.int32
U32 = mybir.dt.uint32
U16 = mybir.dt.uint16
U8 = mybir.dt.uint8
FP8X4 = mybir.dt.float8_e4m3fn_x4
ALU = mybir.AluOpType
ACT = mybir.ActivationFunctionType

P = 128
PACK = 4
S = 512
TABLE = 2048
HALF = S // 2
QUARTER = S // 4
WORDS_PER_LINE = 4
BYTES_PER_LINE = 16
N3_ON_SCALAR = 2

FLOPS = 3 * 2 * S * S * S

AT_W1_SCALE_RAW = 0
AT_D_TABLE = 2 * 1024
AT_W2_SCALE_RAW = 10 * 1024
AT_MEMBERS = 12 * 1024
AT_Z_GROUPED = 20 * 1024
AT_Y = 24 * 1024
AT_W2_RAW = AT_Y + 1024
AT_D_SCALE_TABLE = AT_Y + 5 * 1024


def entries(offsets, first, count):
    return offsets[:, first // 16 : (first + count) // 16]


def words_of(dram_words):
    return dram_words[0].rearrange("p n t -> p (n t)").bitcast(I32)


def deal(copy, dst, src, run):
    copy(
        dst.rearrange("p (t b i) -> p b t i", t=PACK, i=run),
        src.rearrange("p (b i t) -> p b t i", t=PACK, i=run),
    )


def interleave(nc, dst, src):
    nc.vector.tensor_copy(
        dst.rearrange("p (b i) t -> p b t i", i=4),
        src.rearrange("p t (b i) -> p b t i", i=4),
    )


def tile_picked_cdjoingatebghard_none_po_kernel(
    tc, x_words, x_scales, w1_words, w1_scales, gn, w2_words, w2_scales, d_words, d_scales,
    offs, n1, two, k1, n2, n3, out_0, out_1, out_2,
):
    nc = tc.nc
    with ExitStack() as ctx:
        keep = ctx.enter_context(tc.tile_pool(name="keep", bufs=1))
        reuse = ctx.enter_context(tc.tile_pool(name="reuse", bufs=1))
        psum = ctx.enter_context(tc.psum_pool(name="psum", bufs=PACK))

        def sbuf(name, shape, dtype):
            return keep.tile(shape, dtype, name=name, tag=name, align_bytes=64)

        def placed(name, shape, dtype, offset):
            return reuse.tile(shape, dtype, name=name, align_bytes=64, offset=offset)

        def load_list(name, dram_list):
            tile = keep.tile(list(dram_list.shape), U16, name=name)
            nc.sync.dma_start(tile[:], dram_list)
            return tile

        def load_scale_rows(queue, tile, dram_scales, quadrants):
            for q in quadrants:
                queue.dma_start(tile[32 * q : 32 * q + 4, :].bitcast(I32), dram_scales[0, 4 * q : 4 * q + 4, :].bitcast(I32))

        x_scale_table = sbuf("x_scale_table", [P, TABLE], U8)
        w1_scale_raw = placed("w1_scale_raw", [P, S], U8, AT_W1_SCALE_RAW)
        d_scale_table = placed("d_scale_table", [P, TABLE], U8, AT_D_SCALE_TABLE)
        d_scale = sbuf("d_scale", [P, S], U8)
        w2_scale_raw = placed("w2_scale_raw", [P, S], U8, AT_W2_SCALE_RAW)
        nc.gpsimd.memset(x_scale_table[:, : TABLE // 2].bitcast(I32), 0)
        nc.vector.memset(x_scale_table[:, TABLE // 2 :].bitcast(I32), 0)
        nc.vector.memset(d_scale_table[:].bitcast(I32), 0)
        nc.vector.memset(w1_scale_raw[:].bitcast(I32), 0)
        nc.vector.memset(w2_scale_raw[:].bitcast(I32), 0)
        nc.vector.memset(d_scale[:].bitcast(I32), 0)
        warm = sbuf("warm", [P, 16], F32)
        nc.vector.memset(warm[:, 0:1], 0.0)

        offs_sb = load_list("offs_sb", offs)
        two_sb = load_list("two_sb", two)
        load_scale_rows(nc.sync, x_scale_table, x_scales, range(2))
        load_scale_rows(nc.scalar, x_scale_table, x_scales, range(2, 4))
        x_table = sbuf("x_table", [P, TABLE], I32)
        nc.sync.dma_start(x_table[:], words_of(x_words))
        w1_raw = sbuf("w1_raw", [P, S], I32)
        nc.sync.dma_start(w1_raw[:], words_of(w1_words))
        load_scale_rows(nc.sync, w1_scale_raw, w1_scales, range(4))
        w2_raw = placed("w2_raw", [P, S], I32, AT_W2_RAW)
        nc.sync.dma_start(w2_raw[:], words_of(w2_words))
        n1_sb = load_list("n1_sb", n1)
        k1_sb = load_list("k1_sb", k1)
        for e in range(2):
            nc.sync.dma_start(d_scale_table[e:P:16, :].bitcast(I32), d_scales[0, e:16:2, :].bitcast(I32))
        d_table = placed("d_table", [P, TABLE], I32, AT_D_TABLE)
        nc.sync.dma_start(d_table[:], words_of(d_words))
        gain = sbuf("gain", [P, PACK], F32)
        nc.sync.dma_start(gain[:], gn.rearrange("(p t) o -> p (t o)", t=PACK))
        load_scale_rows(nc.sync, w2_scale_raw, w2_scales, range(4))
        n3_sb = load_list("n3_sb", n3)
        n2_sb = load_list("n2_sb", n2)

        nc.scalar.activation(warm[:, 8:9], warm[:, 0:1], ACT.Sigmoid)

        xq_scale = sbuf("xq_scale", [P, S], U8)
        nc.vector.tensor_copy(xq_scale[:], x_scale_table[:].indirect(offs_sb[:]))
        xt_scale = sbuf("xt_scale", [P, S], U8)
        nc.vector.tensor_copy(xt_scale[:], x_scale_table[:].indirect(two_sb[:]))
        xq = sbuf("xq", [P, S], U32)
        nc.vector.tensor_copy(xq[:], x_table[:].bitcast(U32).indirect(offs_sb[:]))
        w1 = sbuf("w1", [P, S], U32)
        deal(nc.scalar.copy, w1[:], w1_raw[:].bitcast(U32), WORDS_PER_LINE)
        w1_scale = sbuf("w1_scale", [P, S], U8)
        deal(nc.vector.tensor_copy, w1_scale[:], w1_scale_raw[:], BYTES_PER_LINE)
        w2 = sbuf("w2", [P, S], U32)
        deal(nc.scalar.copy, w2[:], w2_raw[:].bitcast(U32), WORDS_PER_LINE)
        xt = placed("xt", [P, S], U32, AT_W1_SCALE_RAW)
        nc.vector.tensor_copy(xt[:], x_table[:].bitcast(U32).indirect(two_sb[:]))

        d_scale_picked = sbuf("d_scale_picked", [P, S], U8)
        nc.vector.tensor_copy(d_scale_picked[:], d_scale_table[:].indirect(k1_sb[:]))
        d_scale_dealt = sbuf("d_scale_dealt", [P, S], U8)
        deal(nc.vector.tensor_copy, d_scale_dealt[:], d_scale_picked[:], BYTES_PER_LINE)
        for r in range(4):
            gathered_on = 16 * (r // 2) + r % 2
            nc.sync.dma_start(d_scale[r:P:32, :].bitcast(I32), d_scale_dealt[gathered_on:P:32, :].bitcast(I32))

        def product(bank, t, lhs, lhs_scale, rhs, rhs_scale):
            cols = slice(P * t, P * (t + 1))
            nc.tensor.matmul_mx(
                out=bank, lhsT=lhs[:, cols].bitcast(FP8X4), lhsT_scale=lhs_scale[:, cols],
                rhs=rhs.bitcast(FP8X4), rhs_scale=rhs_scale, start=True, stop=True,
            )

        y = []
        for t in range(PACK):
            bank = psum.tile([P, S], F32, name="first")
            product(bank[:], t, w1, w1_scale, xq[:], xq_scale[:])
            y.append(placed(f"y{t}", [P, S], F32, AT_Y + 2048 * t))
            if t < PACK // 2:
                nc.scalar.copy(y[t][:], bank[:])
            else:
                nc.vector.tensor_copy(y[t][:], bank[:])

        d_picked = sbuf("d_picked", [P, S], U32)
        nc.vector.tensor_copy(d_picked[:], d_table[:].bitcast(U32).indirect(k1_sb[:]))
        d_dealt = sbuf("d_dealt", [P, S], I32)
        deal(nc.vector.tensor_copy, d_dealt[:], d_picked[:].bitcast(I32), WORDS_PER_LINE)
        w2_scale = sbuf("w2_scale", [P, S], U8)
        deal(nc.vector.tensor_copy, w2_scale[:], w2_scale_raw[:], BYTES_PER_LINE)

        members, low, high, gate, diff = {}, {}, {}, {}, {}
        z_rows = [sbuf(f"z_rows{c}", [P, PACK, HALF], BF16) for c in range(2)]

        def fetch_members(c, u):
            members[c, u] = placed(f"members{c}{u}", [P, 2, 2 * HALF], F32, AT_MEMBERS + 4096 * u)
            for e in range(2):
                for h in range(2):
                    nc.scalar.activation(
                        members[c, u][:, e, HALF * h : HALF * (h + 1)],
                        y[2 * u + e][:].indirect(entries(n1_sb, 2 * HALF * c + HALF * h, HALF)), ACT.Copy,
                    )

        def extremes(c, u):
            pair = members[c, u][:].rearrange("p e (j m) -> p (e j) m", m=2)
            if c == 0:
                high[c, u] = placed(f"high{c}{u}", [P, 2 * HALF], F32, AT_D_TABLE + 4096 * u)
                low[c, u] = placed(f"low{c}{u}", [P, 2 * HALF], F32, AT_D_TABLE + 4096 * u + 2048)
            else:
                high[c, u] = sbuf(f"high{c}{u}", [P, 2 * HALF], F32)
                low[c, u] = sbuf(f"low{c}{u}", [P, 2 * HALF], F32)
            nc.vector.tensor_tensor(high[c, u][:], pair[:, :, 0], pair[:, :, 1], ALU.max)
            nc.vector.tensor_tensor(low[c, u][:], pair[:, :, 0], pair[:, :, 1], ALU.min)

        def sigmoid_of_high(c, u):
            gate[c, u] = sbuf(f"gate{c}{u}", [P, 2 * HALF], F32)
            nc.scalar.activation(gate[c, u][:], high[c, u][:], ACT.Sigmoid)

        def subtract_low(c, u):
            if (c, u) == (0, 1):
                diff[c, u] = placed("diff01", [P, 2 * HALF], F32, AT_W2_SCALE_RAW)
            else:
                diff[c, u] = sbuf(f"diff{c}{u}", [P, 2 * HALF], F32)
            for e in range(2):
                part = slice(HALF * e, HALF * (e + 1))
                nc.vector.tensor_tensor(diff[c, u][:, part], y[2 * u + e][:, HALF * c : HALF * (c + 1)], low[c, u][:, part], ALU.subtract)

        def make_z(c, u):
            for e in range(2):
                t, part = 2 * u + e, slice(HALF * e, HALF * (e + 1))
                nc.vector.scalar_tensor_tensor(z_rows[c][:, t, :], diff[c, u][:, part], gain[:, t : t + 1], gate[c, u][:, part], ALU.mult, ALU.mult)

        z_words, z_scale = {}, {}

        def quantise_z(c):
            grouped = placed(f"z_grouped{c}", [P, HALF, PACK], BF16, AT_Z_GROUPED)
            interleave(nc, grouped[:], z_rows[c][:])
            z_words[c] = sbuf(f"z_words{c}", [P, HALF], U32)
            z_scale[c] = sbuf(f"z_scale{c}", [P, HALF], U8)
            nc.vector.quantize_mx(out=z_words[c][:].bitcast(FP8X4), scales=z_scale[c][:], in_=grouped[:].rearrange("p j t -> p (j t)"))

        a = [sbuf(f"a{t}", [P, S], F32) for t in range(PACK)]
        sig_b, picked_sig, gated = {}, {}, {}

        def make_a(c, bank_tag):
            for t in range(PACK):
                bank = psum.tile([P, HALF], F32, name=bank_tag)
                product(bank[:], t, w2, w2_scale, z_words[c][:], z_scale[c][:])
                nc.scalar.copy(a[t][:, HALF * c : HALF * (c + 1)], bank[:])

        def make_sig_b(t):
            bank = psum.tile([P, S], F32, name="second")
            product(bank[:], t, d_dealt, d_scale, xt[:], xt_scale[:])
            sig_b[t] = placed(f"sig_b{t}", [P, S], F32, AT_MEMBERS + 2048 * t)
            nc.scalar.activation(sig_b[t][:], bank[:], ACT.Sigmoid, scale=0.0625)

        def gate_a_fused(c, t):
            nc.vector.tensor_tensor(
                gated[c][:, t, :], sig_b[t][:].indirect(entries(n3_sb, HALF * c, HALF)),
                a[t][:, HALF * c : HALF * (c + 1)], ALU.mult,
            )

        def fetch_sig_b(c, t):
            picked_sig[c, t] = sbuf(f"picked_sig{c}{t}", [P, HALF], F32)
            nc.scalar.activation(picked_sig[c, t][:], sig_b[t][:].indirect(entries(n3_sb, HALF * c, HALF)), ACT.Copy)

        def gate_a_fetched(c, t):
            nc.vector.tensor_tensor(gated[c][:, t, :], picked_sig[c, t][:], a[t][:, HALF * c : HALF * (c + 1)], ALU.mult)

        steps = [(c, u) for c in range(2) for u in range(2)]
        for i in range(len(steps) + 1):
            if i < len(steps):
                fetch_members(*steps[i])
            if i >= 1:
                sigmoid_of_high(*steps[i - 1])
            if i < len(steps):
                extremes(*steps[i])
            if i >= 1:
                make_z(*steps[i - 1])
            if i < len(steps):
                subtract_low(*steps[i])
            if i >= 1 and steps[i - 1] == (0, 1):
                quantise_z(0)
        for t in range(PACK):
            make_sig_b(t)
        make_a(0, "first")
        quantise_z(1)

        gated[0] = placed("gated0", [P, PACK, HALF], F32, AT_Z_GROUPED)
        gated[1] = sbuf("gated1", [P, PACK, HALF], F32)
        for t in range(PACK):
            gate_a_fused(0, t)
        fetch_sig_b(1, 0)
        make_a(1, "second")
        for t in range(1, N3_ON_SCALAR):
            fetch_sig_b(1, t)
        for t in range(N3_ON_SCALAR):
            gate_a_fetched(1, t)
        for t in range(N3_ON_SCALAR, PACK):
            gate_a_fused(1, t)

        out_rows = out_0.rearrange("(p t) j -> p t j", t=PACK)
        out_words = sbuf("out_words", [P, S], U32)
        out_scale = sbuf("out_scale", [P, S], U8)
        out_words_dram = words_of(out_1)
        result, out_grouped = {}, {}
        quarters = S // QUARTER

        def combine(v):
            fetched = sbuf(f"fetched{v}", [P, PACK, QUARTER], F32)
            for t in range(PACK):
                nc.scalar.activation(fetched[:, t, :], a[t][:].indirect(entries(n2_sb, QUARTER * v, QUARTER)), ACT.Copy)
            result[v] = sbuf(f"result{v}", [P, PACK, QUARTER], F32)
            part = slice(QUARTER * (v % 2), QUARTER * (v % 2 + 1))
            nc.vector.scalar_tensor_tensor(result[v][:], fetched[:], -0.5, gated[v // 2][:, :, part], ALU.mult, ALU.add)
            nc.sync.dma_start(out_rows[:, :, QUARTER * v : QUARTER * (v + 1)], result[v][:])

        def group_out(v):
            out_grouped[v] = sbuf(f"out_grouped{v}", [P, QUARTER, PACK], BF16)
            if v == quarters - 2:
                nc.scalar.copy(out_grouped[v][:], result[v][:].rearrange("p t j -> p j t"))
            else:
                interleave(nc, out_grouped[v][:], result[v][:])

        def quantise_out(v):
            cols = slice(QUARTER * v, QUARTER * (v + 1))
            nc.vector.quantize_mx(out=out_words[:, cols].bitcast(FP8X4), scales=out_scale[:, cols], in_=out_grouped[v][:].rearrange("p j t -> p (j t)"))
            if v % 2 == 1:
                half = slice(HALF * (v // 2), HALF * (v // 2 + 1))
                nc.sync.dma_start(out_words_dram[:, half], out_words[:, half].bitcast(I32))

        for v in range(quarters + 1):
            if v < quarters:
                combine(v)
            if v >= 1:
                quantise_out(v - 1)
            if v < quarters:
                group_out(v)
        for q in range(4):
            queue = nc.scalar if q % 2 == 0 else nc.sync
            queue.dma_start(out_2[0, 4 * q : 4 * q + 4, :].bitcast(I32), out_scale[32 * q : 32 * q + 4, :].bitcast(I32))
